import numpy as np, ml_dtypes
CORES = [12,28,60,100,156,228]
N = 6
S, B = 4, 256
def setup_inputs(rng):
    a = (rng.standard_normal((128, 128), dtype=np.float32) / 8).astype(ml_dtypes.bfloat16)
    return {"x": (rng.standard_normal((N, 128, S * B), dtype=np.float32) / 2).astype(ml_dtypes.bfloat16), "a": np.broadcast_to(a, (N, 128, 128)).copy()}
def reference(x, a):
    X, A = x.astype(np.float64), a.astype(np.float64)
    y = np.zeros((N, 128, S * B)); h = np.zeros((128, B))
    for r in range(N):
        for s in range(S):
            h = np.tanh(A[r].T @ h + X[r][:, B * s:B * s + B])
            y[r][:, B * s:B * s + B] = h
    return {"y": y.astype(ml_dtypes.bfloat16)}

from concourse.bass import DstId, RemoteDMATransfer
from concourse.mybir import AluOpType, ActivationFunctionType

S, B = 4, 256
K, W = 4, 64
NR = 6
WORLD = 256

SCRATCH = {
    "a_sb": ("sbuf", [128, 128], "bfloat16"),
    "xraw": ("sbuf", [128, S, K, W], "bfloat16"),
    "xs": ("sbuf", [128, K, S, W], "bfloat16"),
    "rl0": ("sbuf", [128, W], "bfloat16"),
    "rl1": ("sbuf", [128, S - 1, W], "bfloat16"),
    "xin": ("sbuf", [128, NR, S, W], "bfloat16"),
    "h": ("sbuf", [128, NR, S, W], "bfloat16"),
    "ones": ("sbuf", [128, 128], "bfloat16"),
    "ident": ("sbuf", [128, 128], "bfloat16"),
    "land": ("sbuf", [128, K, S, W], "bfloat16"),
    "ysb": ("sbuf", [128, S, K, W], "bfloat16"),
    "ps0": ("psum", [128, 512], "float32"),
    "ps1": ("psum", [128, 512], "float32"),
    "ps2": ("psum", [128, 512], "float32"),
    "ps3": ("psum", [128, 512], "float32"),
}
SEMAPHORES = (["lda", "cpx", "loc", "a", "r0", "r1", "one", "idn", "mm", "act", "cpy", "st"]
              + ["lx%d" % s for s in range(S)] + ["x%d" % i for i in range(NR)]
              + ["xf%d" % i for i in range(NR)] + ["res%d" % k for k in range(K)])


def _bits(mask):
    return [b for b in range(16) if (mask >> b) & 1]


def _mask(bits):
    m = 0
    for b in bits:
        m |= 1 << b
    return m


def _one_chip(topo, a, b):
    return topo.host(a) == topo.host(b) and topo.chip(a) == topo.chip(b)


def _plan(T, topo):
    R = list(T.cores)
    near = [i for i in range(len(R)) if topo.may_write(R[0], R[i])]
    far = [i for i in range(len(R)) if i not in near]

    def owners(i, other):
        return [c for c in range(WORLD) if c != R[i] and _one_chip(topo, c, R[i]) and topo.may_write(c, R[other])]

    workers = []
    for k, i in enumerate(near):
        own = owners(i, far[0])
        same = [c for c in own if topo.die(c) == topo.die(R[i])]
        cross = [c for c in own if topo.die(c) != topo.die(R[i])]
        workers.append((same if k % 2 == 0 else cross)[0])
    relays = {i: owners(i, near[0])[:K] for i in far}
    return R, near, far, workers, relays


def _share_engines(topo, src, workers):
    away = [d for d in workers if not _one_chip(topo, src, d)]
    out_bits = _bits(topo.mask(src, away[0]))
    per = 1
    while per * 2 * len(away) <= len(out_bits):
        per *= 2
    eng, n = [], 0
    for d in workers:
        if _one_chip(topo, src, d):
            eng.append([b for b in _bits(topo.mask(src, d)) if b not in out_bits])
        else:
            eng.append(out_bits[per * n:per * n + per])
            n += 1
    return eng


def _back_engines(topo, worker, R):
    m = 0xFFFF
    for c in R:
        m &= topo.mask(worker, c)
    return _bits(m)


def _xfer(topo, src_core, dst_core, bits, sem, src, dst):
    rid, pid = topo.addr(dst_core, src_core)
    return RemoteDMATransfer(dst_ids=[DstId(rid=rid, pnc=pid)], dma_engine_mask=_mask(bits), remote_sem=sem,
                             src=src, dst=dst)


def _take_back(g, T, topo, R, workers):
    sem = T.sem
    for k in range(K):
        n = len(_back_engines(topo, workers[k], R))
        if k < K - 1:
            g.vector.wait_ge(sem["res%d" % k], n)
            g.vector.tensor_copy(T.ysb[:, :, k, :], T.land[:, k, :, :]).then_inc(sem.cpy, 1)
        else:
            g.scalar.wait_ge(sem["res%d" % k], n)
            g.scalar.activation(T.ysb[:, :, k, :], T.land[:, k, :, :], ActivationFunctionType.Copy).then_inc(sem.cpy, 1)
    g.sync.wait_ge(sem.cpy, K)
    g.sync.dma_start(T.y[:, :], T.ysb[:]).then_inc(sem.st, 16)
    g.sync.wait_ge(sem.st, 16)


def _near_rank(g, core, T, topo, i, R, near, workers):
    sem = T.sem
    mine = workers[near.index(i)]
    g.sync.dma_start(T.a_sb[:], T.a[:, :]).then_inc(sem.lda, 16)
    for s in range(S):
        q = g.scalar if s % 2 == 0 else g.sync
        q.dma_start(T.xraw[:, s], T.x[:, B * s:B * s + B]).then_inc(sem["lx%d" % s], 16)
    for s in range(S):
        g.vector.wait_ge(sem["lx%d" % s], 16)
        g.vector.tensor_copy(T.xs[:, :, s, :], T.xraw[:, s, :, :]).then_inc(sem.cpx, 1)
    abits = _bits(topo.mask(core, mine))
    rid, pid = topo.addr(mine, core)
    g.wait_ge(sem.lda, 16)
    g.remote_dma(out_ap=T.a_sb[:], in_ap=T.a_sb[:], remote_sem=sem.a, local_sem=sem.loc, pid=pid, routing_id=rid,
                 dma_engine_mask=_mask(abits))
    eng = _share_engines(topo, core, workers)
    g.wait_ge(sem.cpx, S)
    g.remote_dma_fused([_xfer(topo, core, workers[k], eng[k], sem["x%d" % i], T.xs[:, k], T.xin[:, i])
                        for k in range(K)], local_sem=sem.loc)
    _take_back(g, T, topo, R, workers)
    g.wait_ge(sem.loc, len(abits) + sum(len(e) for e in eng))


def _relay_engines(topo, src, relays):
    bits = _bits(topo.mask(src, relays[0]))
    per = len(bits) // len(relays)
    return [bits[per * k:per * k + per] for k in range(len(relays))]


def _far_rank(g, core, T, topo, i, R, workers, relays):
    sem = T.sem
    for s in range(S):
        q = g.sync if s % 2 == 0 else g.scalar
        q.dma_start(T.xraw[:, s], T.x[:, B * s:B * s + B]).then_inc(sem["lx%d" % s], 16)
    for s in range(1, S):
        g.vector.wait_ge(sem["lx%d" % s], 16)
        g.vector.tensor_copy(T.xs[:, :, s, :], T.xraw[:, s, :, :]).then_inc(sem.cpx, 1)
    eng = _relay_engines(topo, core, relays)
    g.wait_ge(sem.lx0, 16)
    g.remote_dma_fused([_xfer(topo, core, relays[k], eng[k], sem.r0, T.xraw[:, 0, k, :], T.rl0[:])
                        for k in range(K)], local_sem=sem.loc)
    g.wait_ge(sem.cpx, S - 1)
    g.remote_dma_fused([_xfer(topo, core, relays[k], eng[k], sem.r1, T.xs[:, k, 1:S, :], T.rl1[:])
                        for k in range(K)], local_sem=sem.loc)
    _take_back(g, T, topo, R, workers)
    g.wait_ge(sem.loc, 2 * sum(len(e) for e in eng))


def _relay(g, core, T, topo, i, k, R, workers, relays):
    sem = T.sem
    n_in = len(_relay_engines(topo, R[i], relays)[k])
    bits = _bits(topo.mask(core, workers[k]))
    rid, pid = topo.addr(workers[k], core)
    g.wait_ge(sem.r0, n_in)
    g.remote_dma(out_ap=T.xin[:, i, 0, :], in_ap=T.rl0[:], remote_sem=sem["xf%d" % i], local_sem=sem.loc, pid=pid,
                 routing_id=rid, dma_engine_mask=_mask(bits))
    g.wait_ge(sem.r1, n_in)
    g.remote_dma(out_ap=T.xin[:, i, 1:S, :], in_ap=T.rl1[:], remote_sem=sem["x%d" % i], local_sem=sem.loc, pid=pid,
                 routing_id=rid, dma_engine_mask=_mask(bits))
    g.wait_ge(sem.loc, 2 * len(bits))


def _worker(g, core, T, topo, k, R, near, far, workers, relays):
    sem = T.sem
    te, sc = g.tensor, g.scalar
    banks = [T.ps0, T.ps1, T.ps2, T.ps3]
    steps = len(R) * S
    g.vector.memset(T.ones[:], 1.0).then_inc(sem.one, 1)
    g.wait_ge(sem.one, 1)
    g.affine_select(T.ident[:], T.ones[:], [[-1, 128]], AluOpType.is_equal, 0.0, 0, 1).then_inc(sem.idn, 1)

    def arrived(q, t):
        i, s = t // S, t % S
        if i in near:
            q.wait_ge(sem["x%d" % i], len(_share_engines(topo, R[i], workers)[k]))
        else:
            n = len(_bits(topo.mask(relays[i][k], core)))
            q.wait_ge(sem["xf%d" % i] if s == 0 else sem["x%d" % i], n)

    def put_x(t):
        arrived(te, t)
        te.matmul(banks[t % 4][:, 0:W], T.ident[:], T.xin[:, t // S, t % S, :], True, False)

    arrived(sc, 0)
    sc.activation(T.h[:, 0, 0, :], T.xin[:, 0, 0, :], ActivationFunctionType.Tanh).then_inc(sem.act, 1)
    for t in range(1, steps):
        sc.wait_ge(sem.mm, t)
        sc.activation(T.h[:, t // S, t % S, :], banks[t % 4][:, 0:W], ActivationFunctionType.Tanh).then_inc(sem.act, 1)
    te.wait_ge(sem.idn, 1)
    put_x(1)
    te.wait_ge(sem.a, len(_bits(topo.mask(R[near[k]], core))))
    for t in range(1, steps):
        te.wait_ge(sem.act, t)
        te.matmul(banks[t % 4][:, 0:W], T.a_sb[:], T.h[:, (t - 1) // S, (t - 1) % S, :], False, True).then_inc(sem.mm, 1)
        if t + 1 < steps:
            put_x(t + 1)
    bits = _back_engines(topo, core, R)
    for i in range(len(R)):
        rid, pid = topo.addr(R[i], core)
        g.wait_ge(sem.act, S * i + S)
        g.remote_dma(out_ap=T.land[:, k], in_ap=T.h[:, i], remote_sem=sem["res%d" % k], local_sem=sem.loc, pid=pid,
                     routing_id=rid, dma_engine_mask=_mask(bits))
    g.wait_ge(sem.loc, len(R) * len(bits))


def rank_program(g, core, T, topo):
    R, near, far, workers, relays = _plan(T, topo)
    i = T.rank_of(core)
    if i is not None:
        if i in near:
            _near_rank(g, core, T, topo, i, R, near, workers)
        else:
            _far_rank(g, core, T, topo, i, R, workers, relays[i])
        return
    if core in workers:
        _worker(g, core, T, topo, workers.index(core), R, near, far, workers, relays)
        return
    for j in far:
        if core in relays[j]:
            _relay(g, core, T, topo, j, relays[j].index(core), R, workers, relays[j])
            return
